import numpy as np, ml_dtypes
CORES = [48,51,52,55]
N = 4
BF = ml_dtypes.bfloat16
def f(rng, *shape):
    return (rng.standard_normal(shape, dtype=np.float32) * np.exp2(rng.integers(-2, 3, shape[:-1] + (1,)))).astype(BF)
def wide(rng, *shape):
    v = f(rng, *shape).astype(np.float32); k = shape[:-2] + (1, shape[-1])
    return (v * np.exp2(rng.integers(-6, 7, k)) * (rng.random(k) > 0.0625)).astype(BF)
def gentries(a):
    return np.ascontiguousarray(a.reshape(8, 16, -1).transpose(0, 2, 1)).reshape(8, -1)
def gtable(e):
    e = np.asarray(e); return np.ascontiguousarray(e.reshape(8, -1, 16).transpose(0, 2, 1)).reshape(128, -1).astype(np.int32)
W, F, U, CAP, SW = 3, 256, 4, 32, 3
C = W * F; Z = C + (W - 1) * N * CAP
def pack(x):
    return np.stack([gtable(v.reshape(8, -1)) for v in x])
def unpack(x):
    return np.stack([gentries(v) for v in x])
def sends(rng, full):
    x = np.argsort(rng.random((N, 8, W - 1, N, F)), axis=-1)[..., :CAP] + F * np.arange(W - 1).reshape(1, 1, W - 1, 1, 1)
    n = rng.integers(0, CAP + 1, (N, 8, W - 1, N, 1)); n[0, :, 0, 1] = CAP
    if full: n[:] = CAP
    keep = (np.argsort(rng.random(x.shape), axis=-1) < n) & (np.arange(N).reshape(N, 1, 1, 1, 1) != np.arange(N).reshape(1, 1, 1, N, 1))
    return np.where(keep, x, Z)
def upwind(rng, far, none):
    s = (N, 8, W, U, F); r = np.arange(N).reshape(N, 1, 1, 1, 1); w = np.arange(W).reshape(1, 1, W, 1, 1)
    v = np.where(rng.random(s) < 0.75, w - 1, (rng.random(s) * w).astype(np.int64))
    near = v * F + rng.integers(0, F, s); away = C + (v * N + (r + 1 + rng.integers(0, N - 1, s)) % N) * CAP + rng.integers(0, CAP, s)
    p = rng.random(s)
    return np.where(w == 0, Z, np.where(p < far, away, np.where(p < far + none, Z, near)))
def draw(rng, o, p, x):
    return {"qs": f(rng, N, 128, C), "rm": (0.5 + 0.5 * rng.random((N, 128, C))).astype(BF), "co": (0.75 * rng.random((N, 128, U * C))).astype(BF),
            "sc": (f(rng, N, 16, 16).astype(np.float32) * np.float32(0.0625)).astype(BF), "seq": pack(o), "up": pack(p), "snd": pack(x)}
def orders(rng):
    return np.argsort(rng.random((N, 8, C)), axis=-1)
def setup_inputs(rng):
    return draw(rng, orders(rng), upwind(rng, 0.5, 0.1), sends(rng, False))
def setup_inputs_full(rng):
    return draw(rng, orders(rng), upwind(rng, 0.9, 0.0), sends(rng, True))
def setup_inputs_chain(rng):
    w = np.arange(W).reshape(1, 1, W, 1, 1); r = np.arange(N).reshape(N, 1, 1, 1, 1); x = sends(rng, True)
    p = np.where(w == 0, Z, C + ((w - 1) * N + (r + 1) % N) * CAP + rng.integers(0, CAP, (N, 8, W, U, F)))
    other = np.arange(N).reshape(N, 1, 1, 1) != np.arange(N).reshape(1, 1, 1, N); a = F * np.arange(W - 1).reshape(1, 1, W - 1, 1)
    x[..., 0] = np.where(other, a, Z); x[..., CAP - 1] = np.where(other, a + F - 1, Z)
    return draw(rng, orders(rng), p, x)
def setup_inputs_alike(rng):
    x = sends(rng, True); x[:] = x[..., :1].copy(); p = upwind(rng, 0.5, 0.1); p = np.repeat(p[:, :, :, :1], U, axis=3)
    o = orders(rng); o[:, 0] = np.arange(C); o[:, 1] = np.arange(C)[::-1]; o[:, 3] = o[:, 2]
    return draw(rng, o, p, x)
def setup_inputs_few(rng):
    x = sends(rng, False); k = int(rng.integers(0, N)); x[k] = Z; x[:, :, :, k] = Z
    d = draw(rng, orders(rng), upwind(rng, 0.08, 0.85), x); d["rm"] = np.where(rng.random(d["rm"].shape) < 0.125, np.float32(0), d["rm"].astype(np.float32)).astype(BF)
    return d
def setup_inputs_spread(rng):
    d = setup_inputs(rng); d["qs"] = wide(rng, N, 128, C); return d
def check_inputs(d):
    bad = []
    if not (np.sort(unpack(d["seq"]), axis=-1) == np.arange(C)).all(): bad.append("seq")
    p = unpack(d["up"]).reshape(N, 8, W, U * F).astype(np.int64); w = np.arange(W).reshape(1, 1, W, 1); r = np.arange(N).reshape(N, 1, 1, 1); s = p - C
    if not ((p == Z) | ((p >= 0) & (p < w * F)) | ((s >= 0) & (s < w * N * CAP) & ((s // CAP) % N != r))).all(): bad.append("up")
    x = unpack(d["snd"]).reshape(N, 8, W - 1, N, CAP).astype(np.int64); w = np.arange(W - 1).reshape(1, 1, W - 1, 1, 1)
    other = np.arange(N).reshape(N, 1, 1, 1, 1) != np.arange(N).reshape(1, 1, 1, N, 1)
    if not ((x == Z) | ((x >= w * F) & (x < w * F + F) & other)).all(): bad.append("snd")
    if not all(np.isfinite(d[k].astype(np.float32)).all() for k in ("qs", "rm", "co", "sc")): bad.append("finite")
    return bad
def reference(qs, rm, co, sc, seq, up, snd):
    o = unpack(seq).astype(np.int64); p = unpack(up).astype(np.int64); x = unpack(snd).astype(np.int64)
    src = qs.astype(np.float64).reshape(N, 8, 16, C); rem = rm.astype(np.float64).reshape(N, 8, 16, C); a = co.astype(np.float64).reshape(N, 8, 16, W, U, F)
    s = sc.astype(np.float64).transpose(0, 2, 1); y = np.zeros((N, 16, C), np.float64)
    for k in range(SW):
        win = np.zeros((N, 8, 16, Z + 1), np.float64)
        for w in range(W):
            c = o[:, :, None, w * F:w * F + F]
            h = np.take_along_axis(win, p[:, :, None, w * U * F:(w + 1) * U * F], 3).reshape(N, 8, 16, U, F)
            v = (np.take_along_axis(src, c, 3) + np.sum(a[:, :, :, w] * h, axis=3)) * np.take_along_axis(rem, c, 3)
            win[..., w * F:w * F + F] = v
            if w == W - 1: continue
            for r in range(N):
                for q in range(N):
                    if q == r: continue
                    b = C + (w * N + r) * CAP; e = (w * N + q) * CAP
                    win[q, :, :, b:b + CAP] = np.take_along_axis(win[r], x[r][:, None, e:e + CAP], 2)
        psi = np.zeros((N, 8, 16, C), np.float64); np.put_along_axis(psi, o[:, :, None], win[..., :C], 3)
        flux = np.sum(psi, axis=1); y = y + flux
        src = np.repeat(np.matmul(s, flux)[:, None], 8, axis=1)
    return {"y": y.astype(np.float32)}

@@ -1,0 +1,361 @@
+from concourse.bass import DstId, RemoteDMATransfer
+from concourse.mybir import AluOpType, ActivationFunctionType
+
+SW = 3
+ZC = 512
+SL = 768
+CUT = [(0, 96), (96, 256), (256, 448)]
+XA, XB = 448, 640
+CH = [("ps_s0", 0, 0, 416), ("ps_s1", 0, 416, 656), ("ps_w", 256, 656, 768)]
+NJ = 6
+F32, BF, I32, U16 = "float32", "bfloat16", "int32", "uint16"
+
+
+def buffers(dtype, **cols):
+    return {n: ("sbuf", [128, c], dtype) for n, c in cols.items()}
+
+
+SCRATCH = {n: ("psum", [128, 512], F32) for n in ("ps_s0", "ps_s1", "ps_y0", "ps_y1", "ps_w", "ps_c1", "ps_c2", "ps_c3")}
+SCRATCH.update(buffers(I32, seqi=48, upi=128, sndi=16, upt=64, upz=64))
+SCRATCH.update(buffers(U16, seq16=48, up16=128, ls=12, cmpz=6))
+SCRATCH.update(buffers(BF, qsb=768, rmb=768, cob=2048, scb=16, oneb=128, e2=128))
+SCRATCH.update(buffers(F32, onef=128, idn=128, sct=128, msk=128, iot=768, row=264, win0=1032, win1=1032, c1=XA, c2=XA,
+                       qp=264, rp=264, rps=96, rmp=512, mgz=96, keep=96, run=96, sp1=256, sp2=256, pr1=1032, pr2=1024,
+                       b1=264, b2=256, x2=256, h1=1024 - XA, h2=1024 - XA, g3=96, cb0=776, cb1=776, cb2=776, ysb=192,
+                       sb0=96, sb1=96, sb2=96, sb3=96, sb4=96, sb5=96))
+LOADS = ["seqi", "upi", "sndi", "qsb", "rmb", "co1", "co2", "scb"]
+SEMAPHORES = (["q_v", "q_a", "q_p", "q_g", "sent", "y0", "y1"] + ["ld_" + n for n in LOADS] + ["arr%d" % i for i in range(6)])
+
+
+def plan(src, cores, topo):
+    dst = [c for c in cores if c != src]
+    far = [c for c in dst if topo.die(c) != topo.die(src)]
+    near = [c for c in dst if topo.die(c) == topo.die(src)]
+    return [[(d, topo.engines(src, d)[i::len(grp)]) for i, d in enumerate(grp)] for grp in (far, near) if grp]
+
+
+def rank_program(g, core, T, topo):
+    rank = T.rank_of(core)
+    if rank is None:
+        return
+    A = AluOpType
+    COPY = ActivationFunctionType.Copy
+    cores = list(T.cores)
+    others = [d for d in range(len(cores)) if d != rank]
+    eng = {"v": g.vector, "a": g.scalar, "p": g.tensor, "g": g, "s": g.sync}
+
+    count, hist, clock = {}, {}, {}
+    known = {q: {} for q in eng}
+
+    def need(q, tok):
+        s, c = tok
+        if known[q].get(s, 0) >= c:
+            return
+        eng[q].wait_ge(T.sem[s], c)
+        for s2, c2 in clock.get(tok, {}).items():
+            if known[q].get(s2, 0) < c2:
+                known[q][s2] = c2
+        known[q][s] = c
+
+    def deps(q, reads, writes):
+        toks = {}
+        for lst, w in ((reads, True), (writes, False)):
+            for x in lst:
+                n, lo, hi = x[:3]
+                psum = n[:3] == "ps_"
+                for (l2, h2, kind, tok, q2) in hist.get(n, []):
+                    if psum:
+                        hit = q2 != q or (q != "p" and l2 < hi and lo < h2 and (kind == "w" or not w))
+                    else:
+                        hit = l2 < hi and lo < h2 and (kind == "w" or not w)
+                    if hit and toks.get(tok[0], 0) < tok[1]:
+                        toks[tok[0]] = tok[1]
+        for s in sorted(toks, key=lambda s: -len(clock.get((s, toks[s]), {}))):
+            need(q, (s, toks[s]))
+
+    def note(q, reads, writes, tok):
+        for lst, kind in ((reads, "r"), (writes, "w")):
+            for x in lst:
+                h = hist.setdefault(x[0], [])
+                if kind == "w" and x[0][:3] != "ps_":
+                    h[:] = [e for e in h if not (x[1] <= e[0] and e[1] <= x[2])]
+                h.append((x[1], x[2], kind, tok, q))
+
+    def emit(q, fn, reads, writes, sem=None, n=1):
+        deps(q, reads, writes)
+        s = sem or "q_" + q
+        count[s] = count.get(s, 0) + n
+        fn().then_inc(T.sem[s], n)
+        tok = (s, count[s])
+        c = dict(known[q])
+        c[s] = count[s]
+        clock[tok] = c
+        note(q, reads, writes, tok)
+
+    def ap(x):
+        p = x[3] if len(x) > 3 else 128
+        return T[x[0]][0:p, x[1]:x[2]] if len(x) < 5 else T[x[0]][0:p, x[1]:x[2]:x[4]]
+
+    def ind(w, o):
+        return T[w[0]][:, w[1]:w[2]].indirect(T[o[0]][:, o[1]:o[2]])
+
+    def load(q, sem, dst, src_ap):
+        emit(q, lambda: eng[q].dma_start(ap(dst), src_ap), [], [dst], sem="ld_" + sem, n=16)
+
+    def fill(x, v):
+        emit("v", lambda: g.vector.memset(ap(x), v), [], [x])
+
+    def zeros(x):
+        emit("g", lambda: g.iota(ap(x), [[0, x[2] - x[1]]], 0, 0, allow_small_or_imprecise_dtypes=True), [], [x])
+
+    def tt(out, a, b, op):
+        emit("v", lambda: g.vector.tensor_tensor(ap(out), ap(a), ap(b), op), [a, b], [out])
+
+    def gtt(out, w, o, b, op=A.mult):
+        emit("v", lambda: g.vector.tensor_tensor(ap(out), ind(w, o), ap(b), op), [w, o, b], [out])
+
+    def gv(out, w, o):
+        emit("v", lambda: g.vector.tensor_copy(ap(out), ind(w, o)), [w, o], [out])
+
+    def ga(out, w, o):
+        emit("a", lambda: g.scalar.activation(ap(out), ind(w, o), COPY), [w, o], [out])
+
+    def cpv(out, a):
+        emit("v", lambda: g.vector.tensor_copy(ap(out), ap(a)), [a], [out])
+
+    def cpa(out, a):
+        emit("a", lambda: g.scalar.activation(ap(out), ap(a), COPY), [a], [out])
+
+    def ts(out, a, s1, s2, op0, op1=None):
+        if op1 is None:
+            emit("v", lambda: g.vector.tensor_scalar(ap(out), ap(a), s1, None, op0), [a], [out])
+        else:
+            emit("v", lambda: g.vector.tensor_scalar(ap(out), ap(a), s1, s2, op0, op1), [a], [out])
+
+    def mm(out, l, r, start, stop):
+        emit("p", lambda: g.tensor.matmul(ap(out), ap(l), ap(r), start, stop), [l, r], [out])
+
+    IDN = ("idn", 0, 128)
+
+    def scatter(w, cb, x, y, op):
+        o = ("seq16", 16 * w, 16 * w + 16)
+        emit("v", lambda: g.vector.tensor_tensor(ind((cb, 0, 768), o), ap(x), ap(y), op), [x, y, o], [(cb, 0, 768)])
+
+    def scatter_sum(w, cb):
+        scatter(w, cb, ("b%d" % w, 0, 256), ("pr%d" % w, 768, 1024), A.add)
+
+    def send(k, w):
+        i = 2 * k + w
+        sb = "sb%d" % i
+        deps("g", [(sb, 0, 96)], [])
+        lo = SL + (w * len(cores) + rank) * 32
+        for call in plan(core, cores, topo):
+            tr = []
+            for c, engines in call:
+                j = others.index(cores.index(c))
+                rid, pid = topo.addr(c)[:2]
+                m = 0
+                for e in engines:
+                    m |= 1 << e
+                tr.append(RemoteDMATransfer(dst_ids=[DstId(rid=rid, pnc=pid)], dma_engine_mask=m, remote_sem=T.sem["arr%d" % i],
+                                            src=T[sb][:, 32 * j:32 * j + 32], dst=T["win%d" % (k % 2)][:, lo:lo + 32]))
+                count["sent"] = count.get("sent", 0) + len(engines)
+            g.remote_dma_fused(tr, local_sem=T.sem.sent)
+        tot = sum(len(e) for d in others for call in plan(cores[d], cores, topo) for c, e in call if c == core)
+        for d in others:
+            a = SL + (w * len(cores) + d) * 32
+            note("net", [], [("win%d" % (k % 2), a, a + 32)], ("arr%d" % i, tot))
+
+    load("s", "seqi", ("seqi", 0, 48), T.seq[:, :])
+    load("a", "rmb", ("rmb", 0, 768), T.rm[:, :])
+    load("s", "qsb", ("qsb", 0, 768), T.qs[:, :])
+    load("a", "sndi", ("sndi", 0, 16), T.snd[:, :])
+    load("s", "upi", ("upi", 0, 128), T.up[:, 64:192])
+    load("s", "co1", ("cob", 0, 1024), T.co[:, 1024:2048])
+    load("a", "co2", ("cob", 1024, 2048), T.co[:, 2048:3072])
+    load("s", "scb", ("scb", 0, 16, 16), T.sc[:, :])
+
+    fill(("onef", 0, 128), 1.0)
+    fill(("oneb", 0, 128, 16), 1.0)
+    emit("g", lambda: g.affine_select(T.idn[:, :], T.onef[:, :], [[-1, 128]], A.is_equal, 0.0, 0, 1), [("onef", 0, 128)], [IDN])
+    emit("g", lambda: g.affine_select(T.e2[0:16, :], T.oneb[0:16, :], [[0, 8], [1, 16]], A.is_equal, 0.0, 0, -1),
+         [("oneb", 0, 128)], [("e2", 0, 128)])
+    fill(("qp", 256, 264), 0.0)
+    fill(("rp", 256, 264), 0.0)
+    for b, z in (("win0", lambda x: fill(x, 0.0)), ("win1", zeros)):
+        z((b, 256, SL))
+        z((b, 1024, 1032))
+        for w in (0, 1):
+            lo = SL + (w * len(cores) + rank) * 32
+            z((b, lo, lo + 32))
+    fill(("row", 256, 264), 768.0)
+    fill(("b1", 256, 264), 0.0)
+    fill(("pr1", 1024, 1032), 0.0)
+    fill(("cb1", 768, 776), 0.0)
+    fill(("cb2", 768, 776), 0.0)
+    fill(("keep", 0, 96), 1.0)
+    fill(("keep", 0, 96, 128, 16), 0.0)
+
+    SEQ = [("seq16", 16 * w, 16 * w + 16) for w in range(3)]
+    LS = [("ls", 0, 6), ("ls", 6, 12)]
+    cpv(("seq16", 0, 48), ("seqi", 0, 48))
+
+    def snd_list(w):
+        j = 0
+        while j < 3:
+            n = 1
+            while j + n < 3 and others[j + n] == others[j] + n:
+                n += 1
+            a = 8 * w + 2 * others[j]
+            o, x = ("ls", 6 * w + 2 * j, 6 * w + 2 * (j + n)), ("sndi", a, a + 2 * n)
+            if w:
+                ts(o, x, 512.0, -256.0, A.min, A.add)
+            else:
+                ts(o, x, 256.0, None, A.min)
+            j += n
+
+    ga(("rp", 0, 256), ("rmb", 0, 768), SEQ[0])
+    snd_list(0)
+    ga(("rps", 0, 96), ("rp", 0, 257), LS[0])
+    gv(("qp", 0, 256), ("qsb", 0, 768), SEQ[0])
+    gtt(("sb0", 0, 96), ("qp", 0, 257), LS[0], ("rps", 0, 96))
+    send(0, 0)
+    emit("g", lambda: g.iota(T.iot[:, :], [[1, 768]], 0, 0, allow_small_or_imprecise_dtypes=True), [], [("iot", 0, 768)])
+
+    RMP = [None, ("rmp", 0, 256), ("rmp", 256, 512)]
+    PRM = [None, ("ps_s1", 0, 256), ("ps_y1", 256, 512)]
+    RMC = [(("ps_y0", 0, 512), 0, 512), (("ps_y1", 0, 256), 512, 768)]
+    for p, lo, hi in RMC:
+        cpa(p, ("rmb", lo, hi))
+    ga(RMP[1], ("rmb", 0, 768), SEQ[1])
+    cpa(PRM[1], RMP[1])
+    ts(("upt", 0, 64), ("upi", 0, 64), 1024.0, float(ZC - 1024), A.is_equal, A.mult)
+    tt(("upz", 0, 64), ("upi", 0, 64), ("upt", 0, 64), A.add)
+    cpv(("up16", 0, 64), ("upz", 0, 64))
+    for p, lo, hi in RMC:
+        tt(("cb0", lo, hi), ("qsb", lo, hi), p, A.mult)
+    ga(("win0", 0, 256), ("cb0", 0, 768), SEQ[0])
+    ga(("sp1", 0, 256), ("cb0", 0, 768), SEQ[1])
+
+    def pc(w, i):
+        return ("ps_c%d" % w, 0, 1024 - XB) if i else ("ps_c3", 256 * w - 256, 256 * w - 256 + XB - XA)
+
+    def fold(w):
+        p, c = PRM[w], 1024 * (w - 1)
+        for lo, hi, out in ((0, 256, ("c%d" % w, 0)), (256, XA, ("c%d" % w, 256)), (XA, XB, pc(w, 0)), (XB, 1024, pc(w, 1))):
+            at = lo
+            while at < hi:
+                i = p[1] + at % 256
+                n = min(hi - at, p[2] - i)
+                o = out[1] + at - lo
+                tt((out[0], o, o + n), ("cob", c + at, c + at + n), (p[0], i, i + n), A.mult)
+                at += n
+
+    def presum(w):
+        mm(("ps_w", 0, 256), IDN, ("sp%d" % w, 0, 256), True, False)
+
+    mm(("ps_s0", 0, 128), ("e2", 0, 128, 16), ("e2", 0, 128, 16), True, True)
+    presum(1)
+    fold(1)
+    snd_list(1)
+    cpv(("up16", 64, 128), ("upi", 64, 128))
+
+    def flux(k, h):
+        ps = "ps_y%d" % h
+        n = NJ // 2
+        if k == 0:
+            mm((ps, 0, 32 * n), ("win0", ZC, ZC + 128), ("idn", 0, 32 * n), True, False)
+        for i in range(n):
+            mm((ps, 32 * i, 32 * i + 32), ("cb%d" % k, n * h + i, 768, 128, NJ), ("msk", 0, 32), False, k == SW - 1 and i == n - 1)
+
+    def spare(k):
+        if k > 0:
+            flux(k - 1, 1)
+            return
+        for o in range(8):
+            mm(("ps_s0", 128 + 16 * o, 144 + 16 * o), ("e2", 0, 128, 16), ("scb", 0, 16, 16), True, True)
+        ga(("row", 0, 256), ("iot", 0, 768), SEQ[0])
+        cpa(("msk", 0, 128), ("ps_s0", 0, 128))
+        cpa(("sct", 0, 128), ("ps_s0", 128, 256))
+        cpa(PRM[2], RMP[2])
+
+    def products(w, b, end, k, plain=False):
+        pr, h = "pr%d" % w, "h%d" % w
+
+        def up(lo, hi):
+            return ("up16", 64 * (w - 1) + lo // 16, 64 * (w - 1) + hi // 16)
+
+        ga((h, 0, XB - XA), (b, 0, end), up(XA, XB))
+        ga((h, XB - XA, 1024 - XA), (b, 0, end), up(XB, 1024))
+        for lo, hi in CUT:
+            c = ("cob", 1024 * (w - 1) + lo, 1024 * (w - 1) + hi) if plain else ("c%d" % w, lo, hi)
+            gtt((pr, lo, hi), (b, 0, end), up(lo, hi), c)
+            mm(("ps_w", lo % 256, (hi - 1) % 256 + 1), IDN, (pr, lo, hi), False, False)
+        tt((pr, XA, XB), (h, 0, XB - XA), pc(w, 0), A.mult)
+        mm(("ps_w", XA - 256, 256), IDN, (pr, XA, 512), False, True)
+        tt((pr, XB, 1024), (h, XB - XA, 1024 - XA), pc(w, 1), A.mult)
+        if w == 1:
+            ga(("g3", 0, 96), (pr, 768, 1025), LS[1])
+            cpa(("ps_s0", 256, 512), (pr, 768, 1024))
+        else:
+            if plain:
+                cpa(("ps_s1", 0, 256), (pr, 768, 1024))
+            spare(k)
+        tt(("b%d" % w, 0, 256), (pr, 512, 768), ("ps_w", 0, 256), A.add)
+
+    def wave1(k, b):
+        products(1, b, 896, k)
+        gtt(("sb%d" % (2 * k + 1), 0, 96), ("b1", 0, 257), LS[1], ("g3", 0, 96), A.add)
+        send(k, 1)
+        tt((b, 256, 512), ("b1", 0, 256), ("ps_s0", 256, 512), A.add)
+
+    wave1(0, "win0")
+    ga(("sp2", 0, 256), ("qsb", 0, 768), SEQ[2])
+    ga(RMP[2], ("rmb", 0, 768), SEQ[2])
+    cpa(pc(2, 0), ("cob", 1024 + XA, 1024 + XB))
+    cpa(pc(2, 1), ("cob", 1024 + XB, 2048))
+    presum(2)
+    scatter_sum(1, "cb0")
+    products(2, "win0", 1025, 0, True)
+    tt(("x2", 0, 256), ("b2", 0, 256), ("ps_s1", 0, 256), A.add)
+    scatter(2, "cb0", ("x2", 0, 256), RMP[2], A.mult)
+
+    for k in range(1, SW):
+        b, cb = "win%d" % (k % 2), "cb%d" % k
+        for i, (ps, at, lo, hi) in enumerate(CH):
+            p = (ps, at, at + hi - lo)
+            mm(p, ("sct", 0, 128), ("cb%d" % (k - 1), lo, hi), True, True)
+            if i == 0 and k == 1:
+                gtt(("mgz", 0, 96), ("row", 0, 257), LS[0], ("msk", 0, 96))
+                r, m, x = ("run", 0, 96), ("keep", 0, 96), ("mgz", 0, 96)
+                emit("v", lambda: g.vector.tensor_tensor_scan(ap(r), ap(m), ap(x), 0.0, A.mult, A.add), [m, x], [r])
+                cpv(("cmpz", 0, 6), ("run", 15, 96, 128, 16))
+            tt((cb, lo, hi), p, ("rmb", lo, hi), A.mult)
+        gv(("sb%d" % (2 * k), 0, 96), (cb, 0, 769), ("cmpz", 0, 6))
+        send(k, 0)
+        gv((b, 0, 256), (cb, 0, 768), SEQ[0])
+        for w in (1, 2):
+            ga(("sp%d" % w, 0, 256), (cb, 0, 768), SEQ[w])
+        presum(1)
+        if k == 1:
+            fold(2)
+        wave1(k, b)
+        presum(2)
+        flux(k - 1, 0)
+        scatter_sum(1, cb)
+        products(2, b, 1025, k)
+        scatter_sum(2, cb)
+
+    n = NJ // 2
+    for h in range(2):
+        flux(SW - 1, h)
+        for i in range(n):
+            src, dst = ("ps_y%d" % h, 32 * i, 32 * i + 32), ("ysb", n * h + i, 32 * NJ, 128, NJ)
+            emit("v", lambda: g.vector.transpose(ap(dst), ap(src)), [src], [("piece%d" % (n * h + i), 0, 1)])
+    for a in range(4):
+        q = "sa"[a % 2]
+        lo, hi = 32 * NJ * a, 32 * NJ * (a + 1)
+        emit(q, lambda: eng[q].dma_start(T.y[:, lo:hi], T.ysb[32 * a:32 * a + 16, :]), [("piece%d" % j, 0, 1) for j in range(NJ)],
+             [], sem="y%d" % (a % 2), n=16)
+    for s in ("q_v", "q_a", "q_p", "q_g", "y0", "y1", "sent"):
+        g.wait_ge(T.sem[s], count[s])

@@ -4,10 +4,14 @@ from concourse.mybir import AluOpType, ActivationFunctionType
 SW = 3
 ZC = 512
 SL = 768
+S1 = 1032
+BIG = 2048.0
 CUT = [(0, 96), (96, 256), (256, 448)]
-XA, XB = 448, 640
-CH = [("ps_s0", 0, 0, 416), ("ps_s1", 0, 416, 656), ("ps_w", 256, 656, 768)]
+XA, XB = 448, 768
+NP = 448
+CH = [("ps_s0", 0, 0, 320), ("ps_s1", 0, 320, 576), ("ps_w", 256, 576, 704), ("ps_s0", 0, 704, 768)]
 NJ = 6
+YB = [(0, 4), (4, 6)]
 F32, BF, I32, U16 = "float32", "bfloat16", "int32", "uint16"
 
 
@@ -17,12 +21,12 @@ def buffers(dtype, **cols):
 
 SCRATCH = {n: ("psum", [128, 512], F32) for n in ("ps_s0", "ps_s1", "ps_y0", "ps_y1", "ps_w", "ps_c1", "ps_c2", "ps_c3")}
 SCRATCH.update(buffers(I32, seqi=48, upi=128, sndi=16, upt=64, upz=64))
-SCRATCH.update(buffers(U16, seq16=48, up16=128, ls=12, cmpz=6))
-SCRATCH.update(buffers(BF, qsb=768, rmb=768, cob=2048, scb=16, oneb=128, e2=128))
-SCRATCH.update(buffers(F32, onef=128, idn=128, sct=128, msk=128, iot=768, row=264, win0=1032, win1=1032, c1=XA, c2=XA,
-                       qp=264, rp=264, rps=96, rmp=512, mgz=96, keep=96, run=96, sp1=256, sp2=256, pr1=1032, pr2=1024,
-                       b1=264, b2=256, x2=256, h1=1024 - XA, h2=1024 - XA, g3=96, cb0=776, cb1=776, cb2=776, ysb=192,
-                       sb0=96, sb1=96, sb2=96, sb3=96, sb4=96, sb5=96))
+SCRATCH.update(buffers(U16, seq16=48, up16=128, ls=16, cmp=8))
+SCRATCH.update(buffers(BF, qsb=768, rmb=768, cob=2048, scb=16, e2=128, d16=128, idb=128, rm1=512))
+SCRATCH.update(buffers(F32, onef=128, idn=128, sct=160, step=128, iot=768, row=520, win0=S1 + 136, win1=S1 + 136,
+                       c1=XA, c2=XA, rp=256, rs=128, run=128, sp2=256, pr1=768, p3=520, pr2=1024, b1=520, b2=256,
+                       h1=1024 - XA, h2=1024 - XA, g3=128, cb0=768, cb1=776, cb2=776,
+                       ysb=192, sb0=128, sb1=128, sb2=128, sb3=128, sb4=128, sb5=128))
 LOADS = ["seqi", "upi", "sndi", "qsb", "rmb", "co1", "co2", "scb"]
 SEMAPHORES = (["q_v", "q_a", "q_p", "q_g", "sent", "y0", "y1"] + ["ld_" + n for n in LOADS] + ["arr%d" % i for i in range(6)])
 
@@ -42,9 +46,10 @@ def rank_program(g, core, T, topo):
     COPY = ActivationFunctionType.Copy
     cores = list(T.cores)
     others = [d for d in range(len(cores)) if d != rank]
+    calls = plan(core, cores, topo)
     eng = {"v": g.vector, "a": g.scalar, "p": g.tensor, "g": g, "s": g.sync}
 
-    count, hist, clock = {}, {}, {}
+    count, hist, clock, age = {}, {}, {}, {}
     known = {q: {} for q in eng}
 
     def need(q, tok):
@@ -70,19 +75,21 @@ def rank_program(g, core, T, topo):
                         hit = l2 < hi and lo < h2 and (kind == "w" or not w)
                     if hit and toks.get(tok[0], 0) < tok[1]:
                         toks[tok[0]] = tok[1]
-        for s in sorted(toks, key=lambda s: -len(clock.get((s, toks[s]), {}))):
-            need(q, (s, toks[s]))
+        left = [(s, c) for s, c in toks.items()
+                if not any(s2 != s and clock.get((s2, c2), {}).get(s, 0) >= c for s2, c2 in toks.items())]
+        for tok in sorted(left, key=lambda t: age.get(t, len(age))):
+            need(q, tok)
 
     def note(q, reads, writes, tok):
         for lst, kind in ((reads, "r"), (writes, "w")):
             for x in lst:
                 h = hist.setdefault(x[0], [])
-                if kind == "w" and x[0][:3] != "ps_":
+                if kind == "w" and x[0][:3] != "ps_" and len(x) < 5:
                     h[:] = [e for e in h if not (x[1] <= e[0] and e[1] <= x[2])]
                 h.append((x[1], x[2], kind, tok, q))
 
-    def emit(q, fn, reads, writes, sem=None, n=1):
-        deps(q, reads, writes)
+    def emit(q, fn, reads, writes, sem=None, n=1, free=False):
+        deps(q, reads, [] if free else writes)
         s = sem or "q_" + q
         count[s] = count.get(s, 0) + n
         fn().then_inc(T.sem[s], n)
@@ -90,11 +97,15 @@ def rank_program(g, core, T, topo):
         c = dict(known[q])
         c[s] = count[s]
         clock[tok] = c
+        age[tok] = len(age)
         note(q, reads, writes, tok)
 
     def ap(x):
         p = x[3] if len(x) > 3 else 128
         return T[x[0]][0:p, x[1]:x[2]] if len(x) < 5 else T[x[0]][0:p, x[1]:x[2]:x[4]]
+
+    def cut(x, lo, hi):
+        return (x[0], x[1] + lo, x[1] + hi)
 
     def ind(w, o):
         return T[w[0]][:, w[1]:w[2]].indirect(T[o[0]][:, o[1]:o[2]])
@@ -105,11 +116,14 @@ def rank_program(g, core, T, topo):
     def fill(x, v):
         emit("v", lambda: g.vector.memset(ap(x), v), [], [x])
 
-    def zeros(x):
-        emit("g", lambda: g.iota(ap(x), [[0, x[2] - x[1]]], 0, 0, allow_small_or_imprecise_dtypes=True), [], [x])
+    def iota(x, step, base=0):
+        emit("g", lambda: g.iota(ap(x), [[step, x[2] - x[1]]], base, 0, allow_small_or_imprecise_dtypes=True), [], [x])
 
-    def tt(out, a, b, op):
-        emit("v", lambda: g.vector.tensor_tensor(ap(out), ap(a), ap(b), op), [a, b], [out])
+    def select(out, x, pattern, op, other, base, cm):
+        emit("g", lambda: g.affine_select(ap(out), ap(x), pattern, op, other, base, cm), [x], [out])
+
+    def tt(out, a, b, op, free=False):
+        emit("v", lambda: g.vector.tensor_tensor(ap(out), ap(a), ap(b), op), [a, b], [out], free=free)
 
     def gtt(out, w, o, b, op=A.mult):
         emit("v", lambda: g.vector.tensor_tensor(ap(out), ind(w, o), ap(b), op), [w, o, b], [out])
@@ -137,225 +151,215 @@ def rank_program(g, core, T, topo):
 
     IDN = ("idn", 0, 128)
 
-    def scatter(w, cb, x, y, op):
-        o = ("seq16", 16 * w, 16 * w + 16)
-        emit("v", lambda: g.vector.tensor_tensor(ind((cb, 0, 768), o), ap(x), ap(y), op), [x, y, o], [(cb, 0, 768)])
+    def win(k, lo, hi):
+        return ("win%d" % (k % 2), lo, hi)
 
-    def scatter_sum(w, cb):
-        scatter(w, cb, ("b%d" % w, 0, 256), ("pr%d" % w, 768, 1024), A.add)
+    def cells(k):
+        return ("cb%d" % k, 0, 768)
 
-    def send(k, w):
+    def seq(w):
+        return ("seq16", 16 * w, 16 * w + 16)
+
+    def slots(k, w, d):
+        lo = (SL, S1)[w] + 32 * d
+        return win(k, lo, lo + 32)
+
+    def scatter(k, w, x, y):
+        emit("v", lambda: g.vector.tensor_tensor(ind(cells(k), seq(w)), ap(x), ap(y), A.add), [x, y, seq(w)], [cells(k)])
+
+    def send(k, w, pick):
         i = 2 * k + w
         sb = "sb%d" % i
-        deps("g", [(sb, 0, 96)], [])
-        lo = SL + (w * len(cores) + rank) * 32
-        for call in plan(core, cores, topo):
+        for call in calls:
+            ds = [cores.index(c) for c, engines in call]
+            pick((sb, 32 * min(ds), 32 * max(ds) + 32), min(ds), max(ds) + 1)
+            deps("g", [(sb, 32 * d, 32 * d + 32) for d in ds], [])
             tr = []
-            for c, engines in call:
-                j = others.index(cores.index(c))
+            for d, (c, engines) in zip(ds, call):
                 rid, pid = topo.addr(c)[:2]
                 m = 0
                 for e in engines:
                     m |= 1 << e
                 tr.append(RemoteDMATransfer(dst_ids=[DstId(rid=rid, pnc=pid)], dma_engine_mask=m, remote_sem=T.sem["arr%d" % i],
-                                            src=T[sb][:, 32 * j:32 * j + 32], dst=T["win%d" % (k % 2)][:, lo:lo + 32]))
+                                            src=T[sb][:, 32 * d:32 * d + 32], dst=ap(slots(k, w, rank))))
                 count["sent"] = count.get("sent", 0) + len(engines)
             g.remote_dma_fused(tr, local_sem=T.sem.sent)
         tot = sum(len(e) for d in others for call in plan(cores[d], cores, topo) for c, e in call if c == core)
         for d in others:
-            a = SL + (w * len(cores) + d) * 32
-            note("net", [], [("win%d" % (k % 2), a, a + 32)], ("arr%d" % i, tot))
+            note("net", [], [slots(k, w, d)], ("arr%d" % i, tot))
 
     load("s", "seqi", ("seqi", 0, 48), T.seq[:, :])
-    load("a", "rmb", ("rmb", 0, 768), T.rm[:, :])
+    load("s", "rmb", ("rmb", 0, 768), T.rm[:, :])
     load("s", "qsb", ("qsb", 0, 768), T.qs[:, :])
-    load("a", "sndi", ("sndi", 0, 16), T.snd[:, :])
+    load("s", "sndi", ("sndi", 0, 16), T.snd[:, :])
+    load("s", "scb", ("scb", 0, 16, 16), T.sc[:, :])
     load("s", "upi", ("upi", 0, 128), T.up[:, 64:192])
     load("s", "co1", ("cob", 0, 1024), T.co[:, 1024:2048])
-    load("a", "co2", ("cob", 1024, 2048), T.co[:, 2048:3072])
-    load("s", "scb", ("scb", 0, 16, 16), T.sc[:, :])
+    load("s", "co2", ("cob", 1024, 2048), T.co[:, 2048:3072])
 
+    E2, D16, IDB = ("e2", 0, 128, 16), ("d16", 0, 128, 16), ("idb", 0, 128)
+    QS, RM, SP1, B1 = ("qsb", 0, 768), ("rmb", 0, 768), ("b1", 0, 256), ("b1", 256, 512)
+    P3 = [None, ("p3", 256, 512), ("pr2", 768, 1024)]
     fill(("onef", 0, 128), 1.0)
-    fill(("oneb", 0, 128, 16), 1.0)
-    emit("g", lambda: g.affine_select(T.idn[:, :], T.onef[:, :], [[-1, 128]], A.is_equal, 0.0, 0, 1), [("onef", 0, 128)], [IDN])
-    emit("g", lambda: g.affine_select(T.e2[0:16, :], T.oneb[0:16, :], [[0, 8], [1, 16]], A.is_equal, 0.0, 0, -1),
-         [("oneb", 0, 128)], [("e2", 0, 128)])
-    fill(("qp", 256, 264), 0.0)
-    fill(("rp", 256, 264), 0.0)
-    for b, z in (("win0", lambda x: fill(x, 0.0)), ("win1", zeros)):
-        z((b, 256, SL))
-        z((b, 1024, 1032))
-        for w in (0, 1):
-            lo = SL + (w * len(cores) + rank) * 32
-            z((b, lo, lo + 32))
-    fill(("row", 256, 264), 768.0)
-    fill(("b1", 256, 264), 0.0)
-    fill(("pr1", 1024, 1032), 0.0)
-    fill(("cb1", 768, 776), 0.0)
-    fill(("cb2", 768, 776), 0.0)
-    fill(("keep", 0, 96), 1.0)
-    fill(("keep", 0, 96, 128, 16), 0.0)
+    select(IDB, ("onef", 0, 128), [[-1, 128]], A.is_equal, 0.0, 0, 1)
+    select(IDN, ("onef", 0, 128), [[-1, 128]], A.is_equal, 0.0, 0, 1)
+    select(E2, ("onef", 0, 128, 16), [[0, 8], [1, 16]], A.is_equal, 0.0, 0, -1)
+    fill(win(0, 256, SL), 0.0)
+    fill(D16, BIG)
+    fill(("p3", 0, 520), 0.0)
+    for x in (slots(0, 0, rank), win(0, 896, S1), ("b1", 512, 520)):
+        iota(x, 0)
 
-    SEQ = [("seq16", 16 * w, 16 * w + 16) for w in range(3)]
-    LS = [("ls", 0, 6), ("ls", 6, 12)]
-    cpv(("seq16", 0, 48), ("seqi", 0, 48))
-
-    def snd_list(w):
-        j = 0
-        while j < 3:
-            n = 1
-            while j + n < 3 and others[j + n] == others[j] + n:
-                n += 1
-            a = 8 * w + 2 * others[j]
-            o, x = ("ls", 6 * w + 2 * j, 6 * w + 2 * (j + n)), ("sndi", a, a + 2 * n)
-            if w:
-                ts(o, x, 512.0, -256.0, A.min, A.add)
-            else:
-                ts(o, x, 256.0, None, A.min)
-            j += n
-
-    ga(("rp", 0, 256), ("rmb", 0, 768), SEQ[0])
-    snd_list(0)
-    ga(("rps", 0, 96), ("rp", 0, 257), LS[0])
-    gv(("qp", 0, 256), ("qsb", 0, 768), SEQ[0])
-    gtt(("sb0", 0, 96), ("qp", 0, 257), LS[0], ("rps", 0, 96))
-    send(0, 0)
-    emit("g", lambda: g.iota(T.iot[:, :], [[1, 768]], 0, 0, allow_small_or_imprecise_dtypes=True), [], [("iot", 0, 768)])
-
-    RMP = [None, ("rmp", 0, 256), ("rmp", 256, 512)]
-    PRM = [None, ("ps_s1", 0, 256), ("ps_y1", 256, 512)]
+    RMW = [None, ("rm1", 0, 256), ("rm1", 256, 512)]
+    PRM = [None, ("ps_s1", 0, 512), ("ps_y1", 0, 512)]
     RMC = [(("ps_y0", 0, 512), 0, 512), (("ps_y1", 0, 256), 512, 768)]
-    for p, lo, hi in RMC:
-        cpa(p, ("rmb", lo, hi))
-    ga(RMP[1], ("rmb", 0, 768), SEQ[1])
-    cpa(PRM[1], RMP[1])
-    ts(("upt", 0, 64), ("upi", 0, 64), 1024.0, float(ZC - 1024), A.is_equal, A.mult)
-    tt(("upz", 0, 64), ("upi", 0, 64), ("upt", 0, 64), A.add)
-    cpv(("up16", 0, 64), ("upz", 0, 64))
-    for p, lo, hi in RMC:
-        tt(("cb0", lo, hi), ("qsb", lo, hi), p, A.mult)
-    ga(("win0", 0, 256), ("cb0", 0, 768), SEQ[0])
-    ga(("sp1", 0, 256), ("cb0", 0, 768), SEQ[1])
 
     def pc(w, i):
-        return ("ps_c%d" % w, 0, 1024 - XB) if i else ("ps_c3", 256 * w - 256, 256 * w - 256 + XB - XA)
+        return ("ps_c3", 256 * w - 256, 256 * w) if i else ("ps_c%d" % w, 0, XB - XA)
 
-    def fold(w):
-        p, c = PRM[w], 1024 * (w - 1)
-        for lo, hi, out in ((0, 256, ("c%d" % w, 0)), (256, XA, ("c%d" % w, 256)), (XA, XB, pc(w, 0)), (XB, 1024, pc(w, 1))):
-            at = lo
-            while at < hi:
-                i = p[1] + at % 256
-                n = min(hi - at, p[2] - i)
-                o = out[1] + at - lo
-                tt((out[0], o, o + n), ("cob", c + at, c + at + n), (p[0], i, i + n), A.mult)
-                at += n
+    def fold(w, i):
+        lo, hi, out = ((0, XA, ("c%d" % w, 0, XA)), (XA, XB, pc(w, 0)), (XB, 1024, pc(w, 1)))[i]
+        tt(out, ("cob", 1024 * (w - 1) + lo, 1024 * (w - 1) + hi), cut(PRM[w], lo % 256, lo % 256 + hi - lo), A.mult)
+
+    def twice(w):
+        for i in range(2):
+            mm(cut(PRM[w], 256 * i, 256 * i + 256), IDB, RMW[w], True, True)
+
+    def first(i):
+        p, lo, hi = RMC[i]
+        tt(("cb0", lo, hi), ("qsb", lo, hi), p, A.mult)
 
     def presum(w):
-        mm(("ps_w", 0, 256), IDN, ("sp%d" % w, 0, 256), True, False)
+        mm(("ps_w", 0, 256), IDN, SP1 if w == 1 else ("sp2", 0, 256), True, False)
 
-    mm(("ps_s0", 0, 128), ("e2", 0, 128, 16), ("e2", 0, 128, 16), True, True)
+    cpv(("seq16", 0, 48), ("seqi", 0, 48))
+    ga(("rp", 0, 256), RM, seq(0))
+    ga(RMW[1], RM, seq(1))
+    for p, lo, hi in RMC:
+        mm(p, IDB, ("rmb", lo, hi), True, True)
+    twice(1)
+    gtt(win(0, 0, 256), QS, seq(0), ("rp", 0, 256))
+    ts(("ls", 0, 16), ("sndi", 0, 16), 512.0, None, A.min)
+    send(0, 0, lambda out, lo, hi: gv(out, win(0, 0, 513), ("ls", 2 * lo, 2 * hi)))
+    iota(slots(0, 1, rank), 0)
+    iota(win(0, S1 + 128, S1 + 136), 0)
+    iota(("iot", 0, 768), 1)
+    iota(("row", 256, 520), 0, 768)
+
+    for o in range(8):
+        mm(("ps_s0", 16 * o, 16 * o + 16), E2, ("scb", 0, 16, 16), True, True)
+    mm(("ps_s0", 128, 160), E2, ("e2", 0, 32, 16), True, True)
+    cpa(("sct", 0, 160), ("ps_s0", 0, 160))
+    ga(RMW[2], RM, seq(2))
+    first(0)
+    cpv(("up16", 0, 64), ("upi", 0, 64))
+    first(1)
+    twice(2)
+    ga(SP1, cells(0), seq(1))
     presum(1)
-    fold(1)
-    snd_list(1)
-    cpv(("up16", 64, 128), ("upi", 64, 128))
+    ts(("upt", 0, 64), ("upi", 64, 128), 896.0, float(S1 - 896), A.is_ge, A.mult)
+    fold(1, 0)
+    tt(("upz", 0, 64), ("upi", 64, 128), ("upt", 0, 64), A.add)
+    fold(1, 1)
+    cpv(("up16", 64, 128), ("upz", 0, 64))
+    fold(1, 2)
+    fold(2, 0)
+    fold(2, 2)
 
-    def flux(k, h):
-        ps = "ps_y%d" % h
-        n = NJ // 2
-        if k == 0:
-            mm((ps, 0, 32 * n), ("win0", ZC, ZC + 128), ("idn", 0, 32 * n), True, False)
-        for i in range(n):
-            mm((ps, 32 * i, 32 * i + 32), ("cb%d" % k, n * h + i, 768, 128, NJ), ("msk", 0, 32), False, k == SW - 1 and i == n - 1)
+    def flux(k, j):
+        h = int(j >= YB[1][0])
+        i = j - YB[h][0]
+        mm(("ps_y%d" % h, 32 * i, 32 * i + 32), ("cb%d" % k, j, 768, 128, NJ), ("sct", 128, 160), False,
+           k == SW - 1 and j == YB[h][1] - 1)
 
-    def spare(k):
-        if k > 0:
-            flux(k - 1, 1)
-            return
-        for o in range(8):
-            mm(("ps_s0", 128 + 16 * o, 144 + 16 * o), ("e2", 0, 128, 16), ("scb", 0, 16, 16), True, True)
-        ga(("row", 0, 256), ("iot", 0, 768), SEQ[0])
-        cpa(("msk", 0, 128), ("ps_s0", 0, 128))
-        cpa(("sct", 0, 128), ("ps_s0", 128, 256))
-        cpa(PRM[2], RMP[2])
-
-    def products(w, b, end, k, plain=False):
+    def products(w, k):
         pr, h = "pr%d" % w, "h%d" % w
+        b = win(k, 0, 1025 if w == 1 else S1 + 129)
 
         def up(lo, hi):
             return ("up16", 64 * (w - 1) + lo // 16, 64 * (w - 1) + hi // 16)
 
-        ga((h, 0, XB - XA), (b, 0, end), up(XA, XB))
-        ga((h, XB - XA, 1024 - XA), (b, 0, end), up(XB, 1024))
+        ga((h, 0, XB - XA), b, up(XA, XB))
+        ga((h, XB - XA, 1024 - XA), b, up(XB, 1024))
         for lo, hi in CUT:
-            c = ("cob", 1024 * (w - 1) + lo, 1024 * (w - 1) + hi) if plain else ("c%d" % w, lo, hi)
-            gtt((pr, lo, hi), (b, 0, end), up(lo, hi), c)
-            mm(("ps_w", lo % 256, (hi - 1) % 256 + 1), IDN, (pr, lo, hi), False, False)
-        tt((pr, XA, XB), (h, 0, XB - XA), pc(w, 0), A.mult)
-        mm(("ps_w", XA - 256, 256), IDN, (pr, XA, 512), False, True)
-        tt((pr, XB, 1024), (h, XB - XA, 1024 - XA), pc(w, 1), A.mult)
+            gtt((pr, lo, hi), b, up(lo, hi), ("c%d" % w, lo, hi))
+            e = min(hi, NP)
+            mm(("ps_w", lo % 256, (e - 1) % 256 + 1), IDN, (pr, lo, e), False, e == NP)
+        rest, n = ("ps_c1", NP, 512), NP + 256 - XA
+        tt((pr, XA, NP + 256), (h, 0, n), cut(pc(w, 0), 0, n), A.mult)
+        tt(rest, (h, n, XB - XA), cut(pc(w, 0), n, XB - XA), A.mult)
         if w == 1:
-            ga(("g3", 0, 96), (pr, 768, 1025), LS[1])
-            cpa(("ps_s0", 256, 512), (pr, 768, 1024))
-        else:
-            if plain:
-                cpa(("ps_s1", 0, 256), (pr, 768, 1024))
-            spare(k)
-        tt(("b%d" % w, 0, 256), (pr, 512, 768), ("ps_w", 0, 256), A.add)
+            ga(("sp2", 0, 256), cells(k), seq(2))
+        tt(P3[w], (h, XB - XA, 1024 - XA), pc(w, 1), A.mult)
+        tt((pr, NP + 256, XB), (pr, NP, 512), rest, A.add)
 
-    def wave1(k, b):
-        products(1, b, 896, k)
-        gtt(("sb%d" % (2 * k + 1), 0, 96), ("b1", 0, 257), LS[1], ("g3", 0, 96), A.add)
-        send(k, 1)
-        tt((b, 256, 512), ("b1", 0, 256), ("ps_s0", 256, 512), A.add)
+    PARTS = ((0, NP - 256), (NP - 256, 256))
 
-    wave1(0, "win0")
-    ga(("sp2", 0, 256), ("qsb", 0, 768), SEQ[2])
-    ga(RMP[2], ("rmb", 0, 768), SEQ[2])
-    cpa(pc(2, 0), ("cob", 1024 + XA, 1024 + XB))
-    cpa(pc(2, 1), ("cob", 1024 + XB, 2048))
-    presum(2)
-    scatter_sum(1, "cb0")
-    products(2, "win0", 1025, 0, True)
-    tt(("x2", 0, 256), ("b2", 0, 256), ("ps_s1", 0, 256), A.add)
-    scatter(2, "cb0", ("x2", 0, 256), RMP[2], A.mult)
+    def total(out, w):
+        for lo, hi in PARTS:
+            tt(cut(out, lo, hi), ("pr%d" % w, 512 + lo, 512 + hi), ("ps_w", lo, hi), A.add)
+
+    def wave1(k):
+        products(1, k)
+        ga(("g3", 0, 128), ("p3", 0, 513), ("ls", 8, 16))
+        mm(("ps_s0", 256, 512), IDN, P3[1], True, False)
+        total(B1, 1)
+        send(k, 1, lambda out, lo, hi: gtt(out, ("b1", 0, 513), ("ls", 8 + 2 * lo, 8 + 2 * hi), ("g3", 32 * lo, 32 * hi), A.add))
+        mm(("ps_s0", 256, 512), IDN, B1, False, True)
+        cpa(win(k, 256, 512), ("ps_s0", 256, 512))
+        presum(2)
+
+    wave1(0)
+    select(D16, D16, [[0, 8], [1, 16]], A.is_equal, 0.0, 0, -1)
+    select(D16, D16, [[0, 8], [1, 16]], A.is_ge, -BIG, 0, -1)
+    select(D16, D16, [[0, 8], [-1, 16]], A.is_gt, -2 * BIG, 15, 0)
+    select(D16, D16, [[0, 8], [-1, 16]], A.is_gt, -BIG, 30, -1)
+    for x in (("cb1", 768, 776), ("cb2", 768, 776), win(1, 256, SL), slots(1, 0, rank), win(1, 896, S1), slots(1, 1, rank),
+              win(1, S1 + 128, S1 + 136)):
+        iota(x, 0)
+    fold(2, 1)
+    scatter(0, 1, B1, P3[1])
+    products(2, 0)
+    ga(("row", 0, 256), ("iot", 0, 768), seq(0))
+    ga(("rs", 0, 128), ("row", 0, 513), ("ls", 0, 8))
+    mm(("ps_s0", 0, 128), E2, D16, True, True)
+    cpa(("step", 0, 128), ("ps_s0", 0, 128))
+    total(("b2", 0), 2)
+    scatter(0, 2, ("b2", 0, 256), P3[2])
 
     for k in range(1, SW):
-        b, cb = "win%d" % (k % 2), "cb%d" % k
         for i, (ps, at, lo, hi) in enumerate(CH):
-            p = (ps, at, at + hi - lo)
-            mm(p, ("sct", 0, 128), ("cb%d" % (k - 1), lo, hi), True, True)
-            if i == 0 and k == 1:
-                gtt(("mgz", 0, 96), ("row", 0, 257), LS[0], ("msk", 0, 96))
-                r, m, x = ("run", 0, 96), ("keep", 0, 96), ("mgz", 0, 96)
-                emit("v", lambda: g.vector.tensor_tensor_scan(ap(r), ap(m), ap(x), 0.0, A.mult, A.add), [m, x], [r])
-                cpv(("cmpz", 0, 6), ("run", 15, 96, 128, 16))
-            tt((cb, lo, hi), p, ("rmb", lo, hi), A.mult)
-        gv(("sb%d" % (2 * k), 0, 96), (cb, 0, 769), ("cmpz", 0, 6))
-        send(k, 0)
-        gv((b, 0, 256), (cb, 0, 768), SEQ[0])
-        for w in (1, 2):
-            ga(("sp%d" % w, 0, 256), (cb, 0, 768), SEQ[w])
+            mm((ps, at, at + hi - lo), ("sct", 0, 128), ("cb%d" % (k - 1), lo, hi), True, True)
+            if k == 1 and i == 0:
+                r, x, d = ("run", 0, 128), ("rs", 0, 128), ("step", 0, 128)
+                emit("v", lambda: g.vector.tensor_tensor_scan(ap(r), ap(x), ap(d), -BIG, A.max, A.add), [x, d], [r])
+                ts(("cmp", 0, 8), ("run", 15, 128, 128, 16), BIG + 0.25, None, A.add)
+            tt(("cb%d" % k, lo, hi), (ps, at, at + hi - lo), ("rmb", lo, hi), A.mult)
+        send(k, 0, lambda out, lo, hi: gv(out, ("cb%d" % k, 0, 769), ("cmp", 2 * lo, 2 * hi)))
+        gv(win(k, 0, 256), cells(k), seq(0))
+        ga(SP1, cells(k), seq(1))
         presum(1)
+        wave1(k)
         if k == 1:
-            fold(2)
-        wave1(k, b)
-        presum(2)
-        flux(k - 1, 0)
-        scatter_sum(1, cb)
-        products(2, b, 1025, k)
-        scatter_sum(2, cb)
+            for h, (lo, hi) in enumerate(YB):
+                mm(("ps_y%d" % h, 0, 32 * (hi - lo)), win(0, ZC, ZC + 128), ("idn", 0, 32 * (hi - lo)), True, False)
+        scatter(k, 1, B1, P3[1])
+        products(2, k)
+        for j in range(NJ):
+            flux(k - 1, j)
+        total(("b2", 0), 2)
+        scatter(k, 2, ("b2", 0, 256), P3[2])
 
-    n = NJ // 2
-    for h in range(2):
-        flux(SW - 1, h)
-        for i in range(n):
-            src, dst = ("ps_y%d" % h, 32 * i, 32 * i + 32), ("ysb", n * h + i, 32 * NJ, 128, NJ)
-            emit("v", lambda: g.vector.transpose(ap(dst), ap(src)), [src], [("piece%d" % (n * h + i), 0, 1)])
+    for h, (lo, hi) in enumerate(YB):
+        for j in range(lo, hi):
+            flux(SW - 1, j)
+        for j in range(lo, hi):
+            src, dst = ("ps_y%d" % h, 32 * (j - lo), 32 * (j - lo) + 32), ("ysb", j, 32 * NJ, 128, NJ)
+            emit("v", lambda: g.vector.transpose(ap(dst), ap(src)), [src], [dst], free=True)
     for a in range(4):
         q = "sa"[a % 2]
         lo, hi = 32 * NJ * a, 32 * NJ * (a + 1)
-        emit(q, lambda: eng[q].dma_start(T.y[:, lo:hi], T.ysb[32 * a:32 * a + 16, :]), [("piece%d" % j, 0, 1) for j in range(NJ)],
-             [], sem="y%d" % (a % 2), n=16)
+        emit(q, lambda: eng[q].dma_start(T.y[:, lo:hi], T.ysb[32 * a:32 * a + 16, :]), [("ysb", 0, 32 * NJ)], [],
+             sem="y%d" % (a % 2), n=16)
     for s in ("q_v", "q_a", "q_p", "q_g", "y0", "y1", "sent"):
         g.wait_ge(T.sem[s], count[s])

from concourse.bass import DstId, RemoteDMATransfer
from concourse.mybir import AluOpType, ActivationFunctionType

SW = 3
ZC = 512
SL = 768
S1 = 1032
BIG = 2048.0
CUT = [(0, 96), (96, 256), (256, 448)]
XA, XB = 448, 768
NP = 448
CH = [("ps_s0", 0, 0, 320), ("ps_s1", 0, 320, 576), ("ps_w", 256, 576, 704), ("ps_s0", 0, 704, 768)]
NJ = 6
YB = [(0, 4), (4, 6)]
F32, BF, I32, U16 = "float32", "bfloat16", "int32", "uint16"


def buffers(dtype, **cols):
    return {n: ("sbuf", [128, c], dtype) for n, c in cols.items()}


SCRATCH = {n: ("psum", [128, 512], F32) for n in ("ps_s0", "ps_s1", "ps_y0", "ps_y1", "ps_w", "ps_c1", "ps_c2", "ps_c3")}
SCRATCH.update(buffers(I32, seqi=48, upi=128, sndi=16, upt=64, upz=64))
SCRATCH.update(buffers(U16, seq16=48, up16=128, ls=16, cmp=8))
SCRATCH.update(buffers(BF, qsb=768, rmb=768, cob=2048, scb=16, e2=128, d16=128, idb=128, rm1=512))
SCRATCH.update(buffers(F32, onef=128, idn=128, sct=160, step=128, iot=768, row=520, win0=S1 + 136, win1=S1 + 136,
                       c1=XA, c2=XA, rp=256, rs=128, run=128, sp2=256, pr1=768, p3=520, pr2=1024, b1=520, b2=256,
                       h1=1024 - XA, h2=1024 - XA, g3=128, cb0=768, cb1=776, cb2=776,
                       ysb=192, sb0=128, sb1=128, sb2=128, sb3=128, sb4=128, sb5=128))
LOADS = ["seqi", "upi", "sndi", "qsb", "rmb", "co1", "co2", "scb"]
SEMAPHORES = (["q_v", "q_a", "q_p", "q_g", "sent", "y0", "y1"] + ["ld_" + n for n in LOADS] + ["arr%d" % i for i in range(6)])


def plan(src, cores, topo):
    dst = [c for c in cores if c != src]
    far = [c for c in dst if topo.die(c) != topo.die(src)]
    near = [c for c in dst if topo.die(c) == topo.die(src)]
    return [[(d, topo.engines(src, d)[i::len(grp)]) for i, d in enumerate(grp)] for grp in (far, near) if grp]


def rank_program(g, core, T, topo):
    rank = T.rank_of(core)
    if rank is None:
        return
    A = AluOpType
    COPY = ActivationFunctionType.Copy
    cores = list(T.cores)
    others = [d for d in range(len(cores)) if d != rank]
    calls = plan(core, cores, topo)
    eng = {"v": g.vector, "a": g.scalar, "p": g.tensor, "g": g, "s": g.sync}

    count, hist, clock, age = {}, {}, {}, {}
    known = {q: {} for q in eng}

    def need(q, tok):
        s, c = tok
        if known[q].get(s, 0) >= c:
            return
        eng[q].wait_ge(T.sem[s], c)
        for s2, c2 in clock.get(tok, {}).items():
            if known[q].get(s2, 0) < c2:
                known[q][s2] = c2
        known[q][s] = c

    def deps(q, reads, writes):
        toks = {}
        for lst, w in ((reads, True), (writes, False)):
            for x in lst:
                n, lo, hi = x[:3]
                psum = n[:3] == "ps_"
                for (l2, h2, kind, tok, q2) in hist.get(n, []):
                    if psum:
                        hit = q2 != q or (q != "p" and l2 < hi and lo < h2 and (kind == "w" or not w))
                    else:
                        hit = l2 < hi and lo < h2 and (kind == "w" or not w)
                    if hit and toks.get(tok[0], 0) < tok[1]:
                        toks[tok[0]] = tok[1]
        left = [(s, c) for s, c in toks.items()
                if not any(s2 != s and clock.get((s2, c2), {}).get(s, 0) >= c for s2, c2 in toks.items())]
        for tok in sorted(left, key=lambda t: age.get(t, len(age))):
            need(q, tok)

    def note(q, reads, writes, tok):
        for lst, kind in ((reads, "r"), (writes, "w")):
            for x in lst:
                h = hist.setdefault(x[0], [])
                if kind == "w" and x[0][:3] != "ps_" and len(x) < 5:
                    h[:] = [e for e in h if not (x[1] <= e[0] and e[1] <= x[2])]
                h.append((x[1], x[2], kind, tok, q))

    def emit(q, fn, reads, writes, sem=None, n=1, free=False):
        deps(q, reads, [] if free else writes)
        s = sem or "q_" + q
        count[s] = count.get(s, 0) + n
        fn().then_inc(T.sem[s], n)
        tok = (s, count[s])
        c = dict(known[q])
        c[s] = count[s]
        clock[tok] = c
        age[tok] = len(age)
        note(q, reads, writes, tok)

    def ap(x):
        p = x[3] if len(x) > 3 else 128
        return T[x[0]][0:p, x[1]:x[2]] if len(x) < 5 else T[x[0]][0:p, x[1]:x[2]:x[4]]

    def cut(x, lo, hi):
        return (x[0], x[1] + lo, x[1] + hi)

    def ind(w, o):
        return T[w[0]][:, w[1]:w[2]].indirect(T[o[0]][:, o[1]:o[2]])

    def load(q, sem, dst, src_ap):
        emit(q, lambda: eng[q].dma_start(ap(dst), src_ap), [], [dst], sem="ld_" + sem, n=16)

    def fill(x, v):
        emit("v", lambda: g.vector.memset(ap(x), v), [], [x])

    def iota(x, step, base=0):
        emit("g", lambda: g.iota(ap(x), [[step, x[2] - x[1]]], base, 0, allow_small_or_imprecise_dtypes=True), [], [x])

    def select(out, x, pattern, op, other, base, cm):
        emit("g", lambda: g.affine_select(ap(out), ap(x), pattern, op, other, base, cm), [x], [out])

    def tt(out, a, b, op, free=False):
        emit("v", lambda: g.vector.tensor_tensor(ap(out), ap(a), ap(b), op), [a, b], [out], free=free)

    def gtt(out, w, o, b, op=A.mult):
        emit("v", lambda: g.vector.tensor_tensor(ap(out), ind(w, o), ap(b), op), [w, o, b], [out])

    def gv(out, w, o):
        emit("v", lambda: g.vector.tensor_copy(ap(out), ind(w, o)), [w, o], [out])

    def ga(out, w, o):
        emit("a", lambda: g.scalar.activation(ap(out), ind(w, o), COPY), [w, o], [out])

    def cpv(out, a):
        emit("v", lambda: g.vector.tensor_copy(ap(out), ap(a)), [a], [out])

    def cpa(out, a):
        emit("a", lambda: g.scalar.activation(ap(out), ap(a), COPY), [a], [out])

    def ts(out, a, s1, s2, op0, op1=None):
        if op1 is None:
            emit("v", lambda: g.vector.tensor_scalar(ap(out), ap(a), s1, None, op0), [a], [out])
        else:
            emit("v", lambda: g.vector.tensor_scalar(ap(out), ap(a), s1, s2, op0, op1), [a], [out])

    def mm(out, l, r, start, stop):
        emit("p", lambda: g.tensor.matmul(ap(out), ap(l), ap(r), start, stop), [l, r], [out])

    IDN = ("idn", 0, 128)

    def win(k, lo, hi):
        return ("win%d" % (k % 2), lo, hi)

    def cells(k):
        return ("cb%d" % k, 0, 768)

    def seq(w):
        return ("seq16", 16 * w, 16 * w + 16)

    def slots(k, w, d):
        lo = (SL, S1)[w] + 32 * d
        return win(k, lo, lo + 32)

    def scatter(k, w, x, y):
        emit("v", lambda: g.vector.tensor_tensor(ind(cells(k), seq(w)), ap(x), ap(y), A.add), [x, y, seq(w)], [cells(k)])

    def send(k, w, pick):
        i = 2 * k + w
        sb = "sb%d" % i
        for call in calls:
            ds = [cores.index(c) for c, engines in call]
            pick((sb, 32 * min(ds), 32 * max(ds) + 32), min(ds), max(ds) + 1)
            deps("g", [(sb, 32 * d, 32 * d + 32) for d in ds], [])
            tr = []
            for d, (c, engines) in zip(ds, call):
                rid, pid = topo.addr(c)[:2]
                m = 0
                for e in engines:
                    m |= 1 << e
                tr.append(RemoteDMATransfer(dst_ids=[DstId(rid=rid, pnc=pid)], dma_engine_mask=m, remote_sem=T.sem["arr%d" % i],
                                            src=T[sb][:, 32 * d:32 * d + 32], dst=ap(slots(k, w, rank))))
                count["sent"] = count.get("sent", 0) + len(engines)
            g.remote_dma_fused(tr, local_sem=T.sem.sent)
        tot = sum(len(e) for d in others for call in plan(cores[d], cores, topo) for c, e in call if c == core)
        for d in others:
            note("net", [], [slots(k, w, d)], ("arr%d" % i, tot))

    load("s", "seqi", ("seqi", 0, 48), T.seq[:, :])
    load("s", "rmb", ("rmb", 0, 768), T.rm[:, :])
    load("s", "qsb", ("qsb", 0, 768), T.qs[:, :])
    load("s", "sndi", ("sndi", 0, 16), T.snd[:, :])
    load("s", "scb", ("scb", 0, 16, 16), T.sc[:, :])
    load("s", "upi", ("upi", 0, 128), T.up[:, 64:192])
    load("s", "co1", ("cob", 0, 1024), T.co[:, 1024:2048])
    load("s", "co2", ("cob", 1024, 2048), T.co[:, 2048:3072])

    E2, D16, IDB = ("e2", 0, 128, 16), ("d16", 0, 128, 16), ("idb", 0, 128)
    QS, RM, SP1, B1 = ("qsb", 0, 768), ("rmb", 0, 768), ("b1", 0, 256), ("b1", 256, 512)
    P3 = [None, ("p3", 256, 512), ("pr2", 768, 1024)]
    fill(("onef", 0, 128), 1.0)
    select(IDB, ("onef", 0, 128), [[-1, 128]], A.is_equal, 0.0, 0, 1)
    select(IDN, ("onef", 0, 128), [[-1, 128]], A.is_equal, 0.0, 0, 1)
    select(E2, ("onef", 0, 128, 16), [[0, 8], [1, 16]], A.is_equal, 0.0, 0, -1)
    fill(win(0, 256, SL), 0.0)
    fill(D16, BIG)
    fill(("p3", 0, 520), 0.0)
    for x in (slots(0, 0, rank), win(0, 896, S1), ("b1", 512, 520)):
        iota(x, 0)

    RMW = [None, ("rm1", 0, 256), ("rm1", 256, 512)]
    PRM = [None, ("ps_s1", 0, 512), ("ps_y1", 0, 512)]
    RMC = [(("ps_y0", 0, 512), 0, 512), (("ps_y1", 0, 256), 512, 768)]

    def pc(w, i):
        return ("ps_c3", 256 * w - 256, 256 * w) if i else ("ps_c%d" % w, 0, XB - XA)

    def fold(w, i):
        lo, hi, out = ((0, XA, ("c%d" % w, 0, XA)), (XA, XB, pc(w, 0)), (XB, 1024, pc(w, 1)))[i]
        tt(out, ("cob", 1024 * (w - 1) + lo, 1024 * (w - 1) + hi), cut(PRM[w], lo % 256, lo % 256 + hi - lo), A.mult)

    def twice(w):
        for i in range(2):
            mm(cut(PRM[w], 256 * i, 256 * i + 256), IDB, RMW[w], True, True)

    def first(i):
        p, lo, hi = RMC[i]
        tt(("cb0", lo, hi), ("qsb", lo, hi), p, A.mult)

    def presum(w):
        mm(("ps_w", 0, 256), IDN, SP1 if w == 1 else ("sp2", 0, 256), True, False)

    cpv(("seq16", 0, 48), ("seqi", 0, 48))
    ga(("rp", 0, 256), RM, seq(0))
    ga(RMW[1], RM, seq(1))
    for p, lo, hi in RMC:
        mm(p, IDB, ("rmb", lo, hi), True, True)
    twice(1)
    gtt(win(0, 0, 256), QS, seq(0), ("rp", 0, 256))
    ts(("ls", 0, 16), ("sndi", 0, 16), 512.0, None, A.min)
    send(0, 0, lambda out, lo, hi: gv(out, win(0, 0, 513), ("ls", 2 * lo, 2 * hi)))
    iota(slots(0, 1, rank), 0)
    iota(win(0, S1 + 128, S1 + 136), 0)
    iota(("iot", 0, 768), 1)
    iota(("row", 256, 520), 0, 768)

    for o in range(8):
        mm(("ps_s0", 16 * o, 16 * o + 16), E2, ("scb", 0, 16, 16), True, True)
    mm(("ps_s0", 128, 160), E2, ("e2", 0, 32, 16), True, True)
    cpa(("sct", 0, 160), ("ps_s0", 0, 160))
    ga(RMW[2], RM, seq(2))
    first(0)
    cpv(("up16", 0, 64), ("upi", 0, 64))
    first(1)
    twice(2)
    ga(SP1, cells(0), seq(1))
    presum(1)
    ts(("upt", 0, 64), ("upi", 64, 128), 896.0, float(S1 - 896), A.is_ge, A.mult)
    fold(1, 0)
    tt(("upz", 0, 64), ("upi", 64, 128), ("upt", 0, 64), A.add)
    fold(1, 1)
    cpv(("up16", 64, 128), ("upz", 0, 64))
    fold(1, 2)
    fold(2, 0)
    fold(2, 2)

    def flux(k, j):
        h = int(j >= YB[1][0])
        i = j - YB[h][0]
        mm(("ps_y%d" % h, 32 * i, 32 * i + 32), ("cb%d" % k, j, 768, 128, NJ), ("sct", 128, 160), False,
           k == SW - 1 and j == YB[h][1] - 1)

    def products(w, k):
        pr, h = "pr%d" % w, "h%d" % w
        b = win(k, 0, 1025 if w == 1 else S1 + 129)

        def up(lo, hi):
            return ("up16", 64 * (w - 1) + lo // 16, 64 * (w - 1) + hi // 16)

        ga((h, 0, XB - XA), b, up(XA, XB))
        ga((h, XB - XA, 1024 - XA), b, up(XB, 1024))
        for lo, hi in CUT:
            gtt((pr, lo, hi), b, up(lo, hi), ("c%d" % w, lo, hi))
            e = min(hi, NP)
            mm(("ps_w", lo % 256, (e - 1) % 256 + 1), IDN, (pr, lo, e), False, e == NP)
        rest, n = ("ps_c1", NP, 512), NP + 256 - XA
        tt((pr, XA, NP + 256), (h, 0, n), cut(pc(w, 0), 0, n), A.mult)
        tt(rest, (h, n, XB - XA), cut(pc(w, 0), n, XB - XA), A.mult)
        if w == 1:
            ga(("sp2", 0, 256), cells(k), seq(2))
        tt(P3[w], (h, XB - XA, 1024 - XA), pc(w, 1), A.mult)
        tt((pr, NP + 256, XB), (pr, NP, 512), rest, A.add)

    PARTS = ((0, NP - 256), (NP - 256, 256))

    def total(out, w):
        for lo, hi in PARTS:
            tt(cut(out, lo, hi), ("pr%d" % w, 512 + lo, 512 + hi), ("ps_w", lo, hi), A.add)

    def wave1(k):
        products(1, k)
        ga(("g3", 0, 128), ("p3", 0, 513), ("ls", 8, 16))
        mm(("ps_s0", 256, 512), IDN, P3[1], True, False)
        total(B1, 1)
        send(k, 1, lambda out, lo, hi: gtt(out, ("b1", 0, 513), ("ls", 8 + 2 * lo, 8 + 2 * hi), ("g3", 32 * lo, 32 * hi), A.add))
        mm(("ps_s0", 256, 512), IDN, B1, False, True)
        cpa(win(k, 256, 512), ("ps_s0", 256, 512))
        presum(2)

    wave1(0)
    select(D16, D16, [[0, 8], [1, 16]], A.is_equal, 0.0, 0, -1)
    select(D16, D16, [[0, 8], [1, 16]], A.is_ge, -BIG, 0, -1)
    select(D16, D16, [[0, 8], [-1, 16]], A.is_gt, -2 * BIG, 15, 0)
    select(D16, D16, [[0, 8], [-1, 16]], A.is_gt, -BIG, 30, -1)
    for x in (("cb1", 768, 776), ("cb2", 768, 776), win(1, 256, SL), slots(1, 0, rank), win(1, 896, S1), slots(1, 1, rank),
              win(1, S1 + 128, S1 + 136)):
        iota(x, 0)
    fold(2, 1)
    scatter(0, 1, B1, P3[1])
    products(2, 0)
    ga(("row", 0, 256), ("iot", 0, 768), seq(0))
    ga(("rs", 0, 128), ("row", 0, 513), ("ls", 0, 8))
    mm(("ps_s0", 0, 128), E2, D16, True, True)
    cpa(("step", 0, 128), ("ps_s0", 0, 128))
    total(("b2", 0), 2)
    scatter(0, 2, ("b2", 0, 256), P3[2])

    for k in range(1, SW):
        for i, (ps, at, lo, hi) in enumerate(CH):
            mm((ps, at, at + hi - lo), ("sct", 0, 128), ("cb%d" % (k - 1), lo, hi), True, True)
            if k == 1 and i == 0:
                r, x, d = ("run", 0, 128), ("rs", 0, 128), ("step", 0, 128)
                emit("v", lambda: g.vector.tensor_tensor_scan(ap(r), ap(x), ap(d), -BIG, A.max, A.add), [x, d], [r])
                ts(("cmp", 0, 8), ("run", 15, 128, 128, 16), BIG + 0.25, None, A.add)
            tt(("cb%d" % k, lo, hi), (ps, at, at + hi - lo), ("rmb", lo, hi), A.mult)
        send(k, 0, lambda out, lo, hi: gv(out, ("cb%d" % k, 0, 769), ("cmp", 2 * lo, 2 * hi)))
        gv(win(k, 0, 256), cells(k), seq(0))
        ga(SP1, cells(k), seq(1))
        presum(1)
        wave1(k)
        if k == 1:
            for h, (lo, hi) in enumerate(YB):
                mm(("ps_y%d" % h, 0, 32 * (hi - lo)), win(0, ZC, ZC + 128), ("idn", 0, 32 * (hi - lo)), True, False)
        scatter(k, 1, B1, P3[1])
        products(2, k)
        for j in range(NJ):
            flux(k - 1, j)
        total(("b2", 0), 2)
        scatter(k, 2, ("b2", 0, 256), P3[2])

    for h, (lo, hi) in enumerate(YB):
        for j in range(lo, hi):
            flux(SW - 1, j)
        for j in range(lo, hi):
            src, dst = ("ps_y%d" % h, 32 * (j - lo), 32 * (j - lo) + 32), ("ysb", j, 32 * NJ, 128, NJ)
            emit("v", lambda: g.vector.transpose(ap(dst), ap(src)), [src], [dst], free=True)
    for a in range(4):
        q = "sa"[a % 2]
        lo, hi = 32 * NJ * a, 32 * NJ * (a + 1)
        emit(q, lambda: eng[q].dma_start(T.y[:, lo:hi], T.ysb[32 * a:32 * a + 16, :]), [("ysb", 0, 32 * NJ)], [],
             sem="y%d" % (a % 2), n=16)
    for s in ("q_v", "q_a", "q_p", "q_g", "y0", "y1", "sent"):
        g.wait_ge(T.sem[s], count[s])
